import numpy as np
import ml_dtypes


def mxq(x, axis, fmt="e4m3"):
    dtype, down = {"e4m3": (ml_dtypes.float8_e4m3fn, 7), "e5m2": (ml_dtypes.float8_e5m2, 14)}[fmt]
    v = np.moveaxis(np.asarray(x, np.float32).astype(ml_dtypes.bfloat16).astype(np.float64), axis, -1)
    blocks = v.reshape(v.shape[:-1] + (-1, 32))
    amax = np.abs(blocks).max(-1, keepdims=True)
    byte = np.maximum(np.where(amax > 0, np.frexp(amax)[1] - 1 + 127, 0) - down, 1)
    scale = np.exp2(byte - 127.0)
    codes = (blocks / scale).astype(np.float32).astype(dtype).astype(np.float64)
    return np.moveaxis((codes * scale).reshape(v.shape), -1, axis)


WIDE = False


def mx_kscale(k):
    if not WIDE:
        return np.ones(k)
    levels = np.array([10, -10, 5, -5, 0])
    if k % 512:
        return np.exp2(np.random.permutation(np.resize(levels, k // 32))).repeat(32)
    a = np.empty((k // 512, 16))
    for p in range(k // 512):
        a[p, :8] = np.random.permutation(np.resize(levels, 8))
        for g in range(8):
            far = levels[np.abs(levels - a[p, g]) >= 10]
            a[p, g + 8] = far[np.random.randint(len(far))]
    return np.exp2(a.ravel()).repeat(32)


def f64(x):
    return np.asarray(x).astype(np.float64)


def striped(idx):
    return np.tile(idx.reshape(-1, 16).T, (8, 1)).astype(np.uint16)


def unstriped(offs):
    return offs[:16].T.reshape(-1).astype(np.int64)


def striped8(idx):
    return np.concatenate([x.reshape(-1, 16).T for x in idx]).astype(np.uint16)


def runs(offs, k):
    lists = np.stack([offs[16 * r : 16 * r + 16].T.reshape(-1) for r in range(8)]).astype(np.int64)
    return lists[np.arange(k) % 512 // 64]


def pack_weight(w):
    k, n = w.shape
    w = f64(np.asarray(w, np.float32).astype(ml_dtypes.bfloat16)).reshape(k // 32, 32, n)
    amax = np.abs(w).max(1)
    byte = np.clip(np.where(amax > 0, np.frexp(amax)[1] - 1 + 127 - 7, 1), 1, 254)
    scaled = (w * np.exp2(127.0 - byte)[:, None, :]).reshape(k, n).astype(np.float32)
    words = np.ascontiguousarray(scaled.reshape(k // 512, 128, 4, n).transpose(0, 1, 3, 2)).astype(ml_dtypes.float8_e4m3fn).view(np.uint8)
    return words, np.ascontiguousarray(byte.astype(np.uint8).reshape(k // 512, 16, n))


def unpack_weight(words, scales):
    g, p, n, _ = words.shape
    vals = np.ascontiguousarray(words).view(ml_dtypes.float8_e4m3fn).astype(np.float64) * np.repeat(np.exp2(scales.astype(np.float64) - 127.0), 8, axis=1)[..., None]
    return vals.transpose(0, 1, 3, 2).reshape(g * 512, n)


def sigmoid(v):
    return 1.0 / (1.0 + np.exp(-np.maximum(v, -700.0)))

def planes(y):
    n, m = y.shape
    v = y.astype(np.float32).astype(ml_dtypes.bfloat16).astype(np.float64).reshape(n // 32, 32, m)
    top = np.abs(v).max(1)
    byte = np.clip(np.where(top > 0, np.frexp(top)[1] - 1 + 127 - 7, 1), 1, 254)
    codes = (v * np.exp2(127.0 - byte)[:, None, :]).reshape(n, m).astype(np.float32).astype(ml_dtypes.float8_e4m3fn).view(np.uint8)
    words = codes.reshape(n // 512, 128, 4, m).transpose(0, 1, 3, 2)
    return np.ascontiguousarray(words), np.ascontiguousarray(byte.astype(np.uint8).reshape(n // 512, 16, m))


K, T, S, G, H, W = 512, 1024, 256, 2048, 512, 128


def setup_inputs():
    n = np.random.standard_normal
    s = mx_kscale(K)[:, None]
    packed_xT = pack_weight(n((K, T)) * s)
    packed_dT = pack_weight(n((K, G)) / s)
    perm = np.random.permutation(S)
    perm2 = np.random.permutation(S)
    perm3 = np.random.permutation(S)
    return {
        "x_words": packed_xT[0],
        "x_scales": packed_xT[1],
        "d_words": packed_dT[0],
        "d_scales": packed_dT[1],
        "sl": np.random.uniform(1.0, 2.0, (H, 1)).astype(np.float32),
        "th": (0.5 * n((H, 1))).astype(np.float32),
        "gs": (np.random.uniform(0.5, 1.5, (K, 1)) * s).astype(np.float32),
        "offs": striped(np.random.permutation(T)[:S]),
        "k1": striped8(np.random.randint(0, G, (8, H))),
        "hz": striped8(np.random.randint(0, T, (8, S))),
        "k2": striped8(np.random.randint(0, G, (8, H))),
        "hy": striped8(np.random.randint(0, T, (8, S))),
        "k3": striped8(np.random.randint(0, G, (8, H))),
        "n1": striped(perm[:W]),
        "n2": striped(perm[W:]),
        "n3": striped(perm2[:W]),
        "n4": striped(perm2[W:]),
        "n5": striped(np.random.permutation(S)),
        "k4": striped8(np.random.randint(0, G, (8, H))),
        "k5": striped8(np.random.randint(0, G, (8, H))),
        "two": striped(np.random.permutation(T)[:S]),
        "n6": striped(perm3[:W]),
        "n7": striped(perm3[W:]),
    }


def reference(x_words, x_scales, d_words, d_scales, sl, th, gs, offs, k1, hz, k2, hy, k3, n1, n2, n3, n4, n5, k4, k5, two, n6, n7):
    d_k4 = unpack_weight(d_words, d_scales)[np.arange(K)[:, None], runs(k4, K)]
    d_k1 = unpack_weight(d_words, d_scales)[np.arange(K)[:, None], runs(k1, K)]
    xq = unpack_weight(x_words, x_scales)[:, unstriped(offs)]
    d_k2 = unpack_weight(d_words, d_scales)[np.arange(K)[:, None], runs(k2, K)]
    x_hz = unpack_weight(x_words, x_scales)[np.arange(K)[:, None], runs(hz, K)]
    d_k3 = unpack_weight(d_words, d_scales)[np.arange(K)[:, None], runs(k3, K)]
    x_hy = unpack_weight(x_words, x_scales)[np.arange(K)[:, None], runs(hy, K)]
    h = 0.0625 * (d_k1.T @ xq + d_k2.T @ x_hz + d_k3.T @ x_hy)
    pa = h[:, unstriped(n1)]
    pb = h[:, unstriped(n2)]
    rb = np.minimum(pa, pb)
    ra = np.maximum(pa, pb)
    ua = np.zeros((H, S))
    ua[:, unstriped(n3)] = ra
    ub = ua.copy()
    ub[:, unstriped(n4)] = rb
    sg = sigmoid(f64(sl) * (ub[:, unstriped(n5)] - f64(th)))
    z = f64(gs) * (ub * sg)
    d_k5 = unpack_weight(d_words, d_scales)[np.arange(K)[:, None], runs(k5, K)]
    x_two = unpack_weight(x_words, x_scales)[:, unstriped(two)]
    h2 = 0.0625 * ((d_k4.T @ mxq(z, 0, "e4m3") + d_k5.T @ x_two))
    pa2 = h2[:, unstriped(n6)]
    pb2 = h2[:, unstriped(n7)]
    ra2 = np.maximum(pa2, pb2)
    out = h2.copy()
    out[:, unstriped(n6)] = ra2
    return (out,) + planes(out)

@@ -1,0 +1,262 @@
+from contextlib import ExitStack
+
+import concourse.mybir as mybir
+from concourse.masks import make_identity
+
+K, T, S, G, H, W = 512, 1024, 256, 2048, 512, 128
+FLOPS = 5 * 2 * K * H * S
+
+F32 = mybir.dt.float32
+BF16 = mybir.dt.bfloat16
+I32 = mybir.dt.int32
+U32 = mybir.dt.uint32
+U16 = mybir.dt.uint16
+U8 = mybir.dt.uint8
+FP8X4 = mybir.dt.float8_e4m3fn_x4
+ACT = mybir.ActivationFunctionType
+ALU = mybir.AluOpType
+
+P = 128
+HALF = H // 2
+SIXTEENTH = 0.0625
+
+
+def tile_picked_mthhzmteordfill_none_po_kernel(
+    tc, x_words, x_scales, d_words, d_scales, sl, th, gs, offs, k1, hz, k2, hy, k3,
+    n1, n2, n3, n4, n5, k4, k5, two, n6, n7, out_0, out_1, out_2,
+):
+    nc = tc.nc
+    with ExitStack() as ctx:
+        lists = ctx.enter_context(tc.tile_pool(name="lists", bufs=1))
+        sb = ctx.enter_context(tc.tile_pool(name="sb", bufs=1))
+        ps = ctx.enter_context(tc.psum_pool(name="ps", bufs=1))
+
+        def sbuf(name, shape, dtype, tag=None):
+            return sb.tile(shape, dtype, name=name, tag=tag or name, align_bytes=64)
+
+        def load_list(name, src):
+            t = lists.tile(list(src.shape), U16, name=name)
+            nc.sync.dma_start(t[:], src)
+            return t
+
+        def zero_bytes(t):
+            nc.vector.memset(t[:].bitcast(I32), 0)
+
+        def gather(out, window, offsets):
+            nc.vector.tensor_copy(out, window[:].indirect(offsets))
+
+        def place_scale_rows(queue, plane, picked):
+            for s in range(4):
+                queue.dma_start(plane[s:P:32, :].bitcast(I32), picked[8 * s : P : 32, :].bitcast(I32))
+
+        def mx(out, lw, ls, rw, rs, start, stop):
+            nc.tensor.matmul_mx(out=out, lhsT=lw.bitcast(FP8X4), lhsT_scale=ls, rhs=rw.bitcast(FP8X4), rhs_scale=rs, start=start, stop=stop)
+
+        xs_tab = sbuf("xs_tab", [P, T], U8)
+        ds_tab = sbuf("ds_tab", [P, G], U8)
+        nc.gpsimd.memset(xs_tab[:].bitcast(I32), 0)
+        nc.gpsimd.memset(ds_tab[:].bitcast(I32), 0)
+        nc.scalar.dma_start(xs_tab[0:P:8, :].bitcast(I32), x_scales[0].bitcast(I32))
+        nc.scalar.dma_start(ds_tab[0:P:8, :].bitcast(I32), d_scales[0].bitcast(I32))
+        l_offs = load_list("l_offs", offs)
+        l_hz = load_list("l_hz", hz)
+        l_hy = load_list("l_hy", hy)
+        l_k1 = load_list("l_k1", k1)
+        l_k2 = load_list("l_k2", k2)
+        l_k3 = load_list("l_k3", k3)
+        xw_tab = sbuf("xw_tab", [P, T], U32)
+        dw_tab = sbuf("dw_tab", [P, G], U32)
+        nc.sync.dma_start(xw_tab[:].bitcast(I32), x_words[0].rearrange("p n t -> p (n t)").bitcast(I32))
+        nc.sync.dma_start(dw_tab[:].bitcast(I32), d_words[0].rearrange("p n t -> p (n t)").bitcast(I32))
+
+        plane1 = sbuf("plane1", [P, 3 * S + 3 * HALF], U8)
+        plane2 = sbuf("plane2", [P, 3 * HALF], U8)
+        plane3 = sbuf("plane3", [P, 2 * H + S], U8)
+        for plane in (plane1, plane2, plane3):
+            zero_bytes(plane)
+
+        ident_b = sbuf("ident_b", [P, P], BF16)
+        ident_f = sbuf("ident_f", [P, P], F32)
+        make_identity(nc, ident_b[:])
+        make_identity(nc, ident_f[:])
+
+        x_lists = (l_offs, l_hz, l_hy)
+        k_lists = (l_k1, l_k2, l_k3)
+        hc = HALF // 16
+
+        picked1 = sbuf("picked1", [P, 3 * S + 3 * HALF], U8)
+        for a in range(3):
+            gather(picked1[:, a * S : (a + 1) * S], xs_tab, x_lists[a][:])
+        for a in range(3):
+            gather(picked1[:, 3 * S + a * HALF : 3 * S + (a + 1) * HALF], ds_tab, k_lists[a][:, 0:hc])
+        place_scale_rows(nc.scalar, plane1, picked1)
+
+        rowwise = sbuf("rowwise", [P, 3, 8], F32, tag="picked1")
+        sl_t, th_t, gs_t = (rowwise[:, a, 0:4] for a in range(3))
+        with nc.allow_non_contiguous_dma(reason="one value a row"):
+            for t, src in ((sl_t, sl), (th_t, th), (gs_t, gs)):
+                nc.scalar.dma_start(t, src.rearrange("(t p) o -> p (t o)", p=P))
+
+        l_n1 = load_list("l_n1", n1)
+        l_n2 = load_list("l_n2", n2)
+        l_n3 = load_list("l_n3", n3)
+        l_n4 = load_list("l_n4", n4)
+        l_n5 = load_list("l_n5", n5)
+        l_k4 = load_list("l_k4", k4)
+        l_k5 = load_list("l_k5", k5)
+        l_two = load_list("l_two", two)
+
+        xw = sbuf("xw", [P, 3 * S], U32)
+        for a in range(3):
+            gather(xw[:, a * S : (a + 1) * S], xw_tab, x_lists[a][:])
+        dw0 = [sbuf("dw0_%d" % a, [P, HALF], U32) for a in range(3)]
+        h_ps = [ps.tile([P, S], F32, name="h_ps%d" % t, tag="bank_h", bufs=2) for t in range(2)]
+        for a in range(3):
+            gather(dw0[a][:], dw_tab, k_lists[a][:, 0:hc])
+            for u in range(2):
+                c = 3 * S + a * HALF + u * P
+                mx(h_ps[u][:], dw0[a][:, u * P : (u + 1) * P], plane1[:, c : c + P],
+                   xw[:, a * S : (a + 1) * S], plane1[:, a * S : (a + 1) * S], a == 0, a == 2)
+
+
+        picked2 = sbuf("picked2", [P, 3 * HALF], U8, tag="dw0_0")
+        for a in range(3):
+            gather(picked2[:, a * HALF : (a + 1) * HALF], ds_tab, k_lists[a][:, hc : 2 * hc])
+        place_scale_rows(nc.sync, plane2, picked2)
+        l_n6 = load_list("l_n6", n6)
+        l_n7 = load_list("l_n7", n7)
+
+        z_turned = sbuf("z_turned", [P, 2, 2, P], F32)
+        ranked = {}
+
+        def pair_up(t, bank):
+            h = sbuf("h%d" % t, [P, S], F32)
+            nc.scalar.activation(h[:], bank[:], ACT.Copy, scale=SIXTEENTH)
+            pairs = sbuf("pairs%d" % t, [P, 2 * W], F32)
+            nc.scalar.activation(pairs[:, 0:W], h[:].indirect(l_n1[:]), ACT.Copy)
+            nc.scalar.activation(pairs[:, W : 2 * W], h[:].indirect(l_n2[:]), ACT.Copy)
+            ranked[t] = sbuf("ranked%d" % t, [P, 2 * W], F32)
+            nc.vector.tensor_tensor(ranked[t][:, 0:W], pairs[:, 0:W], pairs[:, W : 2 * W], ALU.max)
+            nc.vector.tensor_tensor(ranked[t][:, W : 2 * W], pairs[:, 0:W], pairs[:, W : 2 * W], ALU.min)
+
+        def gate(t, pieces):
+            ub = sbuf("ub%d" % t, [P, S], F32)
+            nc.scalar.activation(ub[:].indirect(l_n3[:]), ranked[t][:, 0:W], ACT.Copy)
+            nc.scalar.activation(ub[:].indirect(l_n4[:]), ranked[t][:, W : 2 * W], ACT.Copy)
+            sg = sbuf("sg%d" % t, [P, S], F32)
+            for jh in range(2):
+                cols = slice(jh * P, (jh + 1) * P)
+                nc.scalar.activation(sg[:, cols], ub[:].indirect(l_n5[:, 8 * jh : 8 * jh + 8]), ACT.Sigmoid,
+                                     bias=bias_t[:, t : t + 1], scale=sl_t[:, t : t + 1])
+            zs = []
+            for halves in pieces:
+                cols = slice(halves[0] * P, (halves[-1] + 1) * P)
+                z = sbuf("z%d_%d" % (t, halves[0]), [P, len(halves), P], BF16)
+                nc.vector.scalar_tensor_tensor(z[:].rearrange("p h j -> p (h j)"), ub[:, cols], gs_t[:, t : t + 1], sg[:, cols], ALU.mult, ALU.mult)
+                zs.append(z)
+            for halves, z in zip(pieces, zs):
+                turn = ps.tile([P, len(halves), P], BF16, name="turn%d_%d" % (t, halves[0]), tag="bank_h", bufs=2)
+                for i in range(len(halves)):
+                    nc.tensor.transpose(turn[:, i, :], z[:, i, :], ident_b[:])
+                nc.vector.tensor_copy(z_turned[:, halves[0] : halves[-1] + 1, :, 32 * t : 32 * t + 32],
+                                      turn[:].bitcast(F32).rearrange("j h (p u) -> j h u p", u=2))
+
+        whole, split = ((0, 1),), ((0,), (1,))
+        pair_up(0, h_ps[0])
+        bias_t = sbuf("bias_t", [P, 4], F32, tag="h0")
+        nc.vector.scalar_tensor_tensor(bias_t[:], sl_t, -1.0, th_t, ALU.mult, ALU.mult)
+        dw1a = sbuf("dw1a", [P, 2 * HALF], U32, tag="pairs0")
+        for a in range(2):
+            gather(dw1a[:, a * HALF : (a + 1) * HALF], dw_tab, k_lists[a][:, hc : 2 * hc])
+        pair_up(1, h_ps[1])
+        dw1b = sbuf("dw1b", [P, HALF], U32, tag="pairs1")
+        gather(dw1b[:], dw_tab, l_k3[:, hc : 2 * hc])
+        dw1 = (dw1a[:, 0:HALF], dw1a[:, HALF : 2 * HALF], dw1b[:])
+        h_ps2 = [ps.tile([P, S], F32, name="h_ps%d" % t, tag="bank_h", bufs=2) for t in (2, 3)]
+        for a in range(3):
+            for u in range(2):
+                c = a * HALF + u * P
+                mx(h_ps2[u][:], dw1[a][:, u * P : (u + 1) * P], plane2[:, c : c + P],
+                   xw[:, a * S : (a + 1) * S], plane1[:, a * S : (a + 1) * S], a == 0, a == 2)
+
+        gate(0, whole)
+        picked3 = sbuf("picked3", [P, 2 * H + S], U8, tag="ranked0")
+        gather(picked3[:, 0:H], ds_tab, l_k4[:])
+        gather(picked3[:, H : 2 * H], ds_tab, l_k5[:])
+        gather(picked3[:, 2 * H : 2 * H + S], xs_tab, l_two[:])
+        place_scale_rows(nc.sync, plane3, picked3)
+        dw4 = sbuf("dw4", [P, H], U32, tag="sg0")
+        gather(dw4[:], dw_tab, l_k4[:])
+        gate(1, whole)
+        pair_up(2, h_ps2[0])
+        w5 = sbuf("w5", [P, H + S], U32, tag="pairs2")
+        gather(w5[:, 0:H], dw_tab, l_k5[:])
+        gather(w5[:, H : H + S], xw_tab, l_two[:])
+        pair_up(3, h_ps2[1])
+        gate(2, whole)
+
+        def deal(out, src):
+            nc.vector.tensor_copy(out.rearrange("p (t m) -> p m t", t=4), src.rearrange("p (m t) -> p m t", t=4))
+
+        dealt_s = sbuf("dealt_s", [P, 2 * H], U8, tag="ranked2")
+        for a in range(2):
+            deal(dealt_s[:, a * H : (a + 1) * H], plane3[:, a * H : (a + 1) * H])
+        dealt4 = sbuf("dealt4", [P, H], U32, tag="sg2")
+        deal(dealt4[:], dw4[:])
+        gate(3, split)
+        dealt5 = sbuf("dealt5", [P, H], U32, tag="z3_1")
+        deal(dealt5[:], w5[:, 0:H])
+        h2_ps = [ps.tile([P, S], F32, name="h2_ps%d" % t) for t in range(4)]
+
+        z_in = [sbuf("z_in%d" % jh, [P, P, 4], BF16) for jh in range(2)]
+        z_w = sbuf("z_w", [P, S], U32)
+        z_s = sbuf("z_s", [P, S], U8)
+        for jh in range(2):
+            back = ps.tile([P, 2, P], F32, name="back%d" % jh, tag="bank_h", bufs=2)
+            for u in range(2):
+                nc.tensor.transpose(back[:, u, :], z_turned[:, jh, u, :], ident_f[:])
+            words = z_in[jh][:].bitcast(F32)
+            if jh == 0:
+                nc.vector.tensor_copy(words, back[:].rearrange("p u j -> p j u"))
+            else:
+                nc.scalar.copy(words, back[:].rearrange("p u j -> p j u"))
+        for t in range(4):
+            mx(h2_ps[t][:], dealt5[:, t * P : (t + 1) * P], dealt_s[:, H + t * P : H + (t + 1) * P],
+               w5[:, H : H + S], plane3[:, 2 * H : 2 * H + S], True, False)
+        for jh in range(2):
+            cols = slice(jh * P, (jh + 1) * P)
+            nc.vector.quantize_mx(out=z_w[:, cols].bitcast(FP8X4), scales=z_s[:, cols],
+                                  in_=z_in[jh][:].rearrange("p j t -> p (j t)"))
+        for t in range(4):
+            c = slice(t * P, (t + 1) * P)
+            mx(h2_ps[t][:], dealt4[:, c], dealt_s[:, c], z_w[:], z_s[:], False, True)
+
+        y_in = sbuf("y_in", [P, S, 4], BF16)
+        out_rows = out_0.rearrange("(p t) j -> p t j", t=4)
+        ys = []
+        largest = []
+        for t in range(4):
+            h2 = sbuf("h2_%d" % t, [P, S], F32)
+            nc.vector.tensor_scalar(h2[:], h2_ps[t][:], SIXTEENTH, None, ALU.mult)
+            pairs2 = sbuf("pairs2_%d" % t, [P, 2 * W], F32)
+            nc.scalar.activation(pairs2[:, 0:W], h2[:].indirect(l_n6[:]), ACT.Copy)
+            nc.scalar.activation(pairs2[:, W : 2 * W], h2[:].indirect(l_n7[:]), ACT.Copy)
+            y = sbuf("y%d" % t, [P, S], F32)
+            nc.vector.tensor_copy(y[:], h2[:])
+            big = sbuf("big%d" % t, [P, W], F32)
+            nc.vector.tensor_tensor(big[:], pairs2[:, 0:W], pairs2[:, W : 2 * W], ALU.max)
+            ys.append(y)
+            largest.append(big)
+        for t in range(4):
+            nc.scalar.activation(ys[t][:].indirect(l_n6[:]), largest[t][:], ACT.Copy)
+            for cols in ([slice(0, S)] if t < 3 else [slice(0, P), slice(P, S)]):
+                nc.vector.tensor_copy(y_in[:, cols, t], ys[t][:, cols])
+            nc.sync.dma_start(out_rows[:, t, :], ys[t][:])
+        y_w = sbuf("y_w", [P, S], U32)
+        y_s = sbuf("y_s", [P, S], U8)
+        for cols in (slice(0, P), slice(P, S)):
+            nc.vector.quantize_mx(out=y_w[:, cols].bitcast(FP8X4), scales=y_s[:, cols], in_=y_in[:, cols, :].rearrange("p j t -> p (j t)"))
+        nc.sync.dma_start(out_1[0].rearrange("p n t -> p (n t)").bitcast(I32), y_w[:].bitcast(I32))
+        for q in range(4):
+            eng = nc.scalar if q % 2 == 0 else nc.sync
+            eng.dma_start(out_2[0][4 * q : 4 * q + 4, :].bitcast(I32), y_s[32 * q : 32 * q + 4, :].bitcast(I32))

@@ -54,8 +54,8 @@ def tile_picked_mthhzmteordfill_none_po_kernel(
 
         xs_tab = sbuf("xs_tab", [P, T], U8)
         ds_tab = sbuf("ds_tab", [P, G], U8)
-        nc.gpsimd.memset(xs_tab[:].bitcast(I32), 0)
-        nc.gpsimd.memset(ds_tab[:].bitcast(I32), 0)
+        zero_bytes(xs_tab)
+        zero_bytes(ds_tab)
         nc.scalar.dma_start(xs_tab[0:P:8, :].bitcast(I32), x_scales[0].bitcast(I32))
         nc.scalar.dma_start(ds_tab[0:P:8, :].bitcast(I32), d_scales[0].bitcast(I32))
         l_offs = load_list("l_offs", offs)
@@ -96,6 +96,12 @@ def tile_picked_mthhzmteordfill_none_po_kernel(
         with nc.allow_non_contiguous_dma(reason="one value a row"):
             for t, src in ((sl_t, sl), (th_t, th), (gs_t, gs)):
                 nc.scalar.dma_start(t, src.rearrange("(t p) o -> p (t o)", p=P))
+        slope_th = sbuf("slope_th", [P, 4], F32)
+        bias_t = sbuf("bias_t", [P, 4], F32)
+        nc.gpsimd.tensor_tensor(slope_th[:], sl_t, th_t, ALU.mult)
+        nc.gpsimd.tensor_scalar(bias_t[:], slope_th[:], -1.0, 0.0, ALU.mult, ALU.add)
+        warm = sbuf("warm", [P, 1], F32)
+        nc.scalar.activation(warm[:], ident_f[:, 0:1], ACT.Sigmoid)
 
         l_n1 = load_list("l_n1", n1)
         l_n2 = load_list("l_n2", n2)
@@ -110,7 +116,7 @@ def tile_picked_mthhzmteordfill_none_po_kernel(
         for a in range(3):
             gather(xw[:, a * S : (a + 1) * S], xw_tab, x_lists[a][:])
         dw0 = [sbuf("dw0_%d" % a, [P, HALF], U32) for a in range(3)]
-        h_ps = [ps.tile([P, S], F32, name="h_ps%d" % t, tag="bank_h", bufs=2) for t in range(2)]
+        h_ps = [ps.tile([P, S], F32, name="h_ps%d" % t, tag="bank_h", bufs=4) for t in range(2)]
         for a in range(3):
             gather(dw0[a][:], dw_tab, k_lists[a][:, 0:hc])
             for u in range(2):
@@ -123,8 +129,6 @@ def tile_picked_mthhzmteordfill_none_po_kernel(
         for a in range(3):
             gather(picked2[:, a * HALF : (a + 1) * HALF], ds_tab, k_lists[a][:, hc : 2 * hc])
         place_scale_rows(nc.sync, plane2, picked2)
-        l_n6 = load_list("l_n6", n6)
-        l_n7 = load_list("l_n7", n7)
 
         z_turned = sbuf("z_turned", [P, 2, 2, P], F32)
         ranked = {}
@@ -139,105 +143,129 @@ def tile_picked_mthhzmteordfill_none_po_kernel(
             nc.vector.tensor_tensor(ranked[t][:, 0:W], pairs[:, 0:W], pairs[:, W : 2 * W], ALU.max)
             nc.vector.tensor_tensor(ranked[t][:, W : 2 * W], pairs[:, 0:W], pairs[:, W : 2 * W], ALU.min)
 
-        def gate(t, pieces):
-            ub = sbuf("ub%d" % t, [P, S], F32)
-            nc.scalar.activation(ub[:].indirect(l_n3[:]), ranked[t][:, 0:W], ACT.Copy)
-            nc.scalar.activation(ub[:].indirect(l_n4[:]), ranked[t][:, W : 2 * W], ACT.Copy)
-            sg = sbuf("sg%d" % t, [P, S], F32)
-            for jh in range(2):
-                cols = slice(jh * P, (jh + 1) * P)
-                nc.scalar.activation(sg[:, cols], ub[:].indirect(l_n5[:, 8 * jh : 8 * jh + 8]), ACT.Sigmoid,
-                                     bias=bias_t[:, t : t + 1], scale=sl_t[:, t : t + 1])
-            zs = []
-            for halves in pieces:
-                cols = slice(halves[0] * P, (halves[-1] + 1) * P)
-                z = sbuf("z%d_%d" % (t, halves[0]), [P, len(halves), P], BF16)
-                nc.vector.scalar_tensor_tensor(z[:].rearrange("p h j -> p (h j)"), ub[:, cols], gs_t[:, t : t + 1], sg[:, cols], ALU.mult, ALU.mult)
-                zs.append(z)
-            for halves, z in zip(pieces, zs):
-                turn = ps.tile([P, len(halves), P], BF16, name="turn%d_%d" % (t, halves[0]), tag="bank_h", bufs=2)
-                for i in range(len(halves)):
-                    nc.tensor.transpose(turn[:, i, :], z[:, i, :], ident_b[:])
-                nc.vector.tensor_copy(z_turned[:, halves[0] : halves[-1] + 1, :, 32 * t : 32 * t + 32],
-                                      turn[:].bitcast(F32).rearrange("j h (p u) -> j h u p", u=2))
+        ub, sg, z = {}, {}, {}
 
-        whole, split = ((0, 1),), ((0,), (1,))
+        def put_back(t):
+            ub[t] = sbuf("ub%d" % t, [P, S], F32)
+            nc.scalar.activation(ub[t][:].indirect(l_n3[:]), ranked[t][:, 0:W], ACT.Copy)
+            nc.scalar.activation(ub[t][:].indirect(l_n4[:]), ranked[t][:, W : 2 * W], ACT.Copy)
+
+        def gate(t, jh):
+            nc.scalar.activation(sg[t][:, jh * P : (jh + 1) * P], ub[t][:].indirect(l_n5[:, 8 * jh : 8 * jh + 8]), ACT.Sigmoid,
+                                 bias=bias_t[:, t : t + 1], scale=sl_t[:, t : t + 1])
+
+        def weigh(t, jh):
+            z[t, jh] = sbuf("z%d_%d" % (t, jh), [P, P], BF16)
+            nc.vector.scalar_tensor_tensor(z[t, jh][:], ub[t][:, jh * P : (jh + 1) * P], gs_t[:, t : t + 1],
+                                           sg[t][:, jh * P : (jh + 1) * P], ALU.mult, ALU.mult)
+
+        def turn(t0, jh, copy):
+            bank = ps.tile([P, 2, P], BF16, name="turn%d_%d" % (t0, jh), tag="bank_h", bufs=4)
+            for i in range(2):
+                nc.tensor.transpose(bank[:, i, :], z[t0 + i, jh][:], ident_b[:])
+            copy(z_turned[:, jh, :, 32 * t0 : 32 * t0 + 64],
+                 bank[:].rearrange("j i r -> j (i r)").bitcast(F32).rearrange("j (p u) -> j u p", u=2))
+
         pair_up(0, h_ps[0])
-        bias_t = sbuf("bias_t", [P, 4], F32, tag="h0")
-        nc.vector.scalar_tensor_tensor(bias_t[:], sl_t, -1.0, th_t, ALU.mult, ALU.mult)
-        dw1a = sbuf("dw1a", [P, 2 * HALF], U32, tag="pairs0")
-        for a in range(2):
-            gather(dw1a[:, a * HALF : (a + 1) * HALF], dw_tab, k_lists[a][:, hc : 2 * hc])
+        dw1a = sbuf("dw1a", [P, HALF], U32, tag="pairs0")
+        gather(dw1a[:], dw_tab, l_k1[:, hc : 2 * hc])
         pair_up(1, h_ps[1])
-        dw1b = sbuf("dw1b", [P, HALF], U32, tag="pairs1")
-        gather(dw1b[:], dw_tab, l_k3[:, hc : 2 * hc])
-        dw1 = (dw1a[:, 0:HALF], dw1a[:, HALF : 2 * HALF], dw1b[:])
-        h_ps2 = [ps.tile([P, S], F32, name="h_ps%d" % t, tag="bank_h", bufs=2) for t in (2, 3)]
+        dw1b = sbuf("dw1b", [P, 2 * HALF], U32, tag="h1")
+        gather(dw1b[:, 0:HALF], dw_tab, l_k2[:, hc : 2 * hc])
+        gather(dw1b[:, HALF : 2 * HALF], dw_tab, l_k3[:, hc : 2 * hc])
+        dw1 = (dw1a[:], dw1b[:, 0:HALF], dw1b[:, HALF : 2 * HALF])
+        h_ps2 = [ps.tile([P, S], F32, name="h_ps%d" % t, tag="bank_h", bufs=4) for t in (2, 3)]
         for a in range(3):
             for u in range(2):
                 c = a * HALF + u * P
                 mx(h_ps2[u][:], dw1[a][:, u * P : (u + 1) * P], plane2[:, c : c + P],
                    xw[:, a * S : (a + 1) * S], plane1[:, a * S : (a + 1) * S], a == 0, a == 2)
 
-        gate(0, whole)
+        put_back(0)
         picked3 = sbuf("picked3", [P, 2 * H + S], U8, tag="ranked0")
         gather(picked3[:, 0:H], ds_tab, l_k4[:])
         gather(picked3[:, H : 2 * H], ds_tab, l_k5[:])
         gather(picked3[:, 2 * H : 2 * H + S], xs_tab, l_two[:])
         place_scale_rows(nc.sync, plane3, picked3)
-        dw4 = sbuf("dw4", [P, H], U32, tag="sg0")
-        gather(dw4[:], dw_tab, l_k4[:])
-        gate(1, whole)
+        l_n6 = load_list("l_n6", n6)
+        l_n7 = load_list("l_n7", n7)
+        put_back(1)
+        xw_two = sbuf("xw_two", [P, S], U32, tag="ranked1")
+        gather(xw_two[:], xw_tab, l_two[:])
         pair_up(2, h_ps2[0])
-        w5 = sbuf("w5", [P, H + S], U32, tag="pairs2")
-        gather(w5[:, 0:H], dw_tab, l_k5[:])
-        gather(w5[:, H : H + S], xw_tab, l_two[:])
         pair_up(3, h_ps2[1])
-        gate(2, whole)
+        dw4 = sbuf("dw4", [P, H], U32, tag="pairs2")
+        gather(dw4[:], dw_tab, l_k4[:])
+        sg[0] = sbuf("sg0", [P, S], F32, tag="h2")
+        sg[1] = sbuf("sg1", [P, S], F32, tag="h3")
+        for jh in range(2):
+            for t in (0, 1):
+                gate(t, jh)
+                weigh(t, jh)
+        for jh in range(2):
+            turn(0, jh, nc.vector.tensor_copy)
+        dw5 = sbuf("dw5", [P, H], U32, tag="h3")
+        gather(dw5[:], dw_tab, l_k5[:])
+        put_back(2)
+        put_back(3)
+        sg[2] = sbuf("sg2", [P, S], F32)
+        sg[3] = sbuf("sg3", [P, S], F32)
+        for jh in range(2):
+            for t in (2, 3):
+                gate(t, jh)
+                weigh(t, jh)
+        turn(2, 0, nc.vector.tensor_copy)
+        turn(2, 1, nc.scalar.copy)
 
-        def deal(out, src):
-            nc.vector.tensor_copy(out.rearrange("p (t m) -> p m t", t=4), src.rearrange("p (m t) -> p m t", t=4))
+        def deal_scales(half, tag):
+            scales = sbuf("dealt_s%d" % half, [P, 2, 2, P], U8, tag=tag)
+            nc.vector.tensor_copy(scales[:].rearrange("p a t m -> p a m t"),
+                                  plane3[:, 0 : 2 * H].rearrange("p (a m t) -> p a m t", a=2, t=4)[:, :, :, 2 * half : 2 * half + 2])
+            return scales
 
-        dealt_s = sbuf("dealt_s", [P, 2 * H], U8, tag="ranked2")
-        for a in range(2):
-            deal(dealt_s[:, a * H : (a + 1) * H], plane3[:, a * H : (a + 1) * H])
-        dealt4 = sbuf("dealt4", [P, H], U32, tag="sg2")
-        deal(dealt4[:], dw4[:])
-        gate(3, split)
-        dealt5 = sbuf("dealt5", [P, H], U32, tag="z3_1")
-        deal(dealt5[:], w5[:, 0:H])
-        h2_ps = [ps.tile([P, S], F32, name="h2_ps%d" % t) for t in range(4)]
+        def deal_words(half, tag):
+            words = sbuf("dealt_w%d" % half, [P, 2, 2, P], U32, tag=tag)
+            for a, picked in ((1, dw5), (0, dw4)):
+                nc.vector.tensor_copy(words[:, a, :, :].rearrange("p t m -> p m t"),
+                                      picked[:].rearrange("p (m t) -> p m t", t=4)[:, :, 2 * half : 2 * half + 2])
+            return words
 
         z_in = [sbuf("z_in%d" % jh, [P, P, 4], BF16) for jh in range(2)]
         z_w = sbuf("z_w", [P, S], U32)
         z_s = sbuf("z_s", [P, S], U8)
         for jh in range(2):
-            back = ps.tile([P, 2, P], F32, name="back%d" % jh, tag="bank_h", bufs=2)
+            back = ps.tile([P, 2, P], F32, name="back%d" % jh, tag="bank_h", bufs=4)
             for u in range(2):
                 nc.tensor.transpose(back[:, u, :], z_turned[:, jh, u, :], ident_f[:])
-            words = z_in[jh][:].bitcast(F32)
-            if jh == 0:
-                nc.vector.tensor_copy(words, back[:].rearrange("p u j -> p j u"))
-            else:
-                nc.scalar.copy(words, back[:].rearrange("p u j -> p j u"))
-        for t in range(4):
-            mx(h2_ps[t][:], dealt5[:, t * P : (t + 1) * P], dealt_s[:, H + t * P : H + (t + 1) * P],
-               w5[:, H : H + S], plane3[:, 2 * H : 2 * H + S], True, False)
+            nc.scalar.copy(z_in[jh][:].bitcast(F32), back[:].rearrange("p u j -> p j u"))
+        scales0 = deal_scales(0, "sg3")
+        words0 = deal_words(0, "ub3")
         for jh in range(2):
             cols = slice(jh * P, (jh + 1) * P)
             nc.vector.quantize_mx(out=z_w[:, cols].bitcast(FP8X4), scales=z_s[:, cols],
                                   in_=z_in[jh][:].rearrange("p j t -> p (j t)"))
-        for t in range(4):
-            c = slice(t * P, (t + 1) * P)
-            mx(h2_ps[t][:], dealt4[:, c], dealt_s[:, c], z_w[:], z_s[:], False, True)
+        h2_ps = [ps.tile([P, S], F32, name="h2_ps%d" % t) for t in range(4)]
+
+        def second_products(half, words, scales):
+            for i in range(2):
+                mx(h2_ps[2 * half + i][:], words[:, 1, i, :], scales[:, 1, i, :],
+                   xw_two[:], plane3[:, 2 * H : 2 * H + S], True, False)
+            for jh in range(2):
+                cols = slice(jh * P, (jh + 1) * P)
+                for i in range(2):
+                    mx(h2_ps[2 * half + i][:, cols], words[:, 0, i, :], scales[:, 0, i, :], z_w[:, cols], z_s[:, cols], False, jh == 1)
 
         y_in = sbuf("y_in", [P, S, 4], BF16)
         out_rows = out_0.rearrange("(p t) j -> p t j", t=4)
         ys = []
         largest = []
-        for t in range(4):
+
+        def pair_up_again(t):
             h2 = sbuf("h2_%d" % t, [P, S], F32)
-            nc.vector.tensor_scalar(h2[:], h2_ps[t][:], SIXTEENTH, None, ALU.mult)
+            if t == 0:
+                nc.scalar.activation(h2[:], h2_ps[t][:], ACT.Copy, scale=SIXTEENTH)
+            else:
+                nc.vector.tensor_scalar(h2[:], h2_ps[t][:], SIXTEENTH, None, ALU.mult)
             pairs2 = sbuf("pairs2_%d" % t, [P, 2 * W], F32)
             nc.scalar.activation(pairs2[:, 0:W], h2[:].indirect(l_n6[:]), ACT.Copy)
             nc.scalar.activation(pairs2[:, W : 2 * W], h2[:].indirect(l_n7[:]), ACT.Copy)
@@ -247,6 +275,15 @@ def tile_picked_mthhzmteordfill_none_po_kernel(
             nc.vector.tensor_tensor(big[:], pairs2[:, 0:W], pairs2[:, W : 2 * W], ALU.max)
             ys.append(y)
             largest.append(big)
+
+        second_products(0, words0, scales0)
+        words1 = deal_words(1, "z_in1")
+        pair_up_again(0)
+        pair_up_again(1)
+        scales1 = deal_scales(1, "sg3")
+        second_products(1, words1, scales1)
+        pair_up_again(2)
+        pair_up_again(3)
         for t in range(4):
             nc.scalar.activation(ys[t][:].indirect(l_n6[:]), largest[t][:], ACT.Copy)
             for cols in ([slice(0, S)] if t < 3 else [slice(0, P), slice(P, S)]):
@@ -256,7 +293,7 @@ def tile_picked_mthhzmteordfill_none_po_kernel(
         y_s = sbuf("y_s", [P, S], U8)
         for cols in (slice(0, P), slice(P, S)):
             nc.vector.quantize_mx(out=y_w[:, cols].bitcast(FP8X4), scales=y_s[:, cols], in_=y_in[:, cols, :].rearrange("p j t -> p (j t)"))
-        nc.sync.dma_start(out_1[0].rearrange("p n t -> p (n t)").bitcast(I32), y_w[:].bitcast(I32))
+            nc.sync.dma_start(out_1[0].rearrange("p n t -> p (n t)").bitcast(I32)[:, cols], y_w[:, cols].bitcast(I32))
         for q in range(4):
             eng = nc.scalar if q % 2 == 0 else nc.sync
             eng.dma_start(out_2[0][4 * q : 4 * q + 4, :].bitcast(I32), y_s[32 * q : 32 * q + 4, :].bitcast(I32))

from contextlib import ExitStack

import concourse.mybir as mybir
from concourse.masks import make_identity

K, T, S, G, H, W = 512, 1024, 256, 2048, 512, 128
FLOPS = 5 * 2 * K * H * S

F32 = mybir.dt.float32
BF16 = mybir.dt.bfloat16
I32 = mybir.dt.int32
U32 = mybir.dt.uint32
U16 = mybir.dt.uint16
U8 = mybir.dt.uint8
FP8X4 = mybir.dt.float8_e4m3fn_x4
ACT = mybir.ActivationFunctionType
ALU = mybir.AluOpType

P = 128
HALF = H // 2
SIXTEENTH = 0.0625


def tile_picked_mthhzmteordfill_none_po_kernel(
    tc, x_words, x_scales, d_words, d_scales, sl, th, gs, offs, k1, hz, k2, hy, k3,
    n1, n2, n3, n4, n5, k4, k5, two, n6, n7, out_0, out_1, out_2,
):
    nc = tc.nc
    with ExitStack() as ctx:
        lists = ctx.enter_context(tc.tile_pool(name="lists", bufs=1))
        sb = ctx.enter_context(tc.tile_pool(name="sb", bufs=1))
        ps = ctx.enter_context(tc.psum_pool(name="ps", bufs=1))

        def sbuf(name, shape, dtype, tag=None):
            return sb.tile(shape, dtype, name=name, tag=tag or name, align_bytes=64)

        def load_list(name, src):
            t = lists.tile(list(src.shape), U16, name=name)
            nc.sync.dma_start(t[:], src)
            return t

        def zero_bytes(t):
            nc.vector.memset(t[:].bitcast(I32), 0)

        def gather(out, window, offsets):
            nc.vector.tensor_copy(out, window[:].indirect(offsets))

        def place_scale_rows(queue, plane, picked):
            for s in range(4):
                queue.dma_start(plane[s:P:32, :].bitcast(I32), picked[8 * s : P : 32, :].bitcast(I32))

        def mx(out, lw, ls, rw, rs, start, stop):
            nc.tensor.matmul_mx(out=out, lhsT=lw.bitcast(FP8X4), lhsT_scale=ls, rhs=rw.bitcast(FP8X4), rhs_scale=rs, start=start, stop=stop)

        xs_tab = sbuf("xs_tab", [P, T], U8)
        ds_tab = sbuf("ds_tab", [P, G], U8)
        zero_bytes(xs_tab)
        zero_bytes(ds_tab)
        nc.scalar.dma_start(xs_tab[0:P:8, :].bitcast(I32), x_scales[0].bitcast(I32))
        nc.scalar.dma_start(ds_tab[0:P:8, :].bitcast(I32), d_scales[0].bitcast(I32))
        l_offs = load_list("l_offs", offs)
        l_hz = load_list("l_hz", hz)
        l_hy = load_list("l_hy", hy)
        l_k1 = load_list("l_k1", k1)
        l_k2 = load_list("l_k2", k2)
        l_k3 = load_list("l_k3", k3)
        xw_tab = sbuf("xw_tab", [P, T], U32)
        dw_tab = sbuf("dw_tab", [P, G], U32)
        nc.sync.dma_start(xw_tab[:].bitcast(I32), x_words[0].rearrange("p n t -> p (n t)").bitcast(I32))
        nc.sync.dma_start(dw_tab[:].bitcast(I32), d_words[0].rearrange("p n t -> p (n t)").bitcast(I32))

        plane1 = sbuf("plane1", [P, 3 * S + 3 * HALF], U8)
        plane2 = sbuf("plane2", [P, 3 * HALF], U8)
        plane3 = sbuf("plane3", [P, 2 * H + S], U8)
        for plane in (plane1, plane2, plane3):
            zero_bytes(plane)

        ident_b = sbuf("ident_b", [P, P], BF16)
        ident_f = sbuf("ident_f", [P, P], F32)
        make_identity(nc, ident_b[:])
        make_identity(nc, ident_f[:])

        x_lists = (l_offs, l_hz, l_hy)
        k_lists = (l_k1, l_k2, l_k3)
        hc = HALF // 16

        picked1 = sbuf("picked1", [P, 3 * S + 3 * HALF], U8)
        for a in range(3):
            gather(picked1[:, a * S : (a + 1) * S], xs_tab, x_lists[a][:])
        for a in range(3):
            gather(picked1[:, 3 * S + a * HALF : 3 * S + (a + 1) * HALF], ds_tab, k_lists[a][:, 0:hc])
        place_scale_rows(nc.scalar, plane1, picked1)

        rowwise = sbuf("rowwise", [P, 3, 8], F32, tag="picked1")
        sl_t, th_t, gs_t = (rowwise[:, a, 0:4] for a in range(3))
        with nc.allow_non_contiguous_dma(reason="one value a row"):
            for t, src in ((sl_t, sl), (th_t, th), (gs_t, gs)):
                nc.scalar.dma_start(t, src.rearrange("(t p) o -> p (t o)", p=P))
        slope_th = sbuf("slope_th", [P, 4], F32)
        bias_t = sbuf("bias_t", [P, 4], F32)
        nc.gpsimd.tensor_tensor(slope_th[:], sl_t, th_t, ALU.mult)
        nc.gpsimd.tensor_scalar(bias_t[:], slope_th[:], -1.0, 0.0, ALU.mult, ALU.add)
        warm = sbuf("warm", [P, 1], F32)
        nc.scalar.activation(warm[:], ident_f[:, 0:1], ACT.Sigmoid)

        l_n1 = load_list("l_n1", n1)
        l_n2 = load_list("l_n2", n2)
        l_n3 = load_list("l_n3", n3)
        l_n4 = load_list("l_n4", n4)
        l_n5 = load_list("l_n5", n5)
        l_k4 = load_list("l_k4", k4)
        l_k5 = load_list("l_k5", k5)
        l_two = load_list("l_two", two)

        xw = sbuf("xw", [P, 3 * S], U32)
        for a in range(3):
            gather(xw[:, a * S : (a + 1) * S], xw_tab, x_lists[a][:])
        dw0 = [sbuf("dw0_%d" % a, [P, HALF], U32) for a in range(3)]
        h_ps = [ps.tile([P, S], F32, name="h_ps%d" % t, tag="bank_h", bufs=4) for t in range(2)]
        for a in range(3):
            gather(dw0[a][:], dw_tab, k_lists[a][:, 0:hc])
            for u in range(2):
                c = 3 * S + a * HALF + u * P
                mx(h_ps[u][:], dw0[a][:, u * P : (u + 1) * P], plane1[:, c : c + P],
                   xw[:, a * S : (a + 1) * S], plane1[:, a * S : (a + 1) * S], a == 0, a == 2)


        picked2 = sbuf("picked2", [P, 3 * HALF], U8, tag="dw0_0")
        for a in range(3):
            gather(picked2[:, a * HALF : (a + 1) * HALF], ds_tab, k_lists[a][:, hc : 2 * hc])
        place_scale_rows(nc.sync, plane2, picked2)

        z_turned = sbuf("z_turned", [P, 2, 2, P], F32)
        ranked = {}

        def pair_up(t, bank):
            h = sbuf("h%d" % t, [P, S], F32)
            nc.scalar.activation(h[:], bank[:], ACT.Copy, scale=SIXTEENTH)
            pairs = sbuf("pairs%d" % t, [P, 2 * W], F32)
            nc.scalar.activation(pairs[:, 0:W], h[:].indirect(l_n1[:]), ACT.Copy)
            nc.scalar.activation(pairs[:, W : 2 * W], h[:].indirect(l_n2[:]), ACT.Copy)
            ranked[t] = sbuf("ranked%d" % t, [P, 2 * W], F32)
            nc.vector.tensor_tensor(ranked[t][:, 0:W], pairs[:, 0:W], pairs[:, W : 2 * W], ALU.max)
            nc.vector.tensor_tensor(ranked[t][:, W : 2 * W], pairs[:, 0:W], pairs[:, W : 2 * W], ALU.min)

        ub, sg, z = {}, {}, {}

        def put_back(t):
            ub[t] = sbuf("ub%d" % t, [P, S], F32)
            nc.scalar.activation(ub[t][:].indirect(l_n3[:]), ranked[t][:, 0:W], ACT.Copy)
            nc.scalar.activation(ub[t][:].indirect(l_n4[:]), ranked[t][:, W : 2 * W], ACT.Copy)

        def gate(t, jh):
            nc.scalar.activation(sg[t][:, jh * P : (jh + 1) * P], ub[t][:].indirect(l_n5[:, 8 * jh : 8 * jh + 8]), ACT.Sigmoid,
                                 bias=bias_t[:, t : t + 1], scale=sl_t[:, t : t + 1])

        def weigh(t, jh):
            z[t, jh] = sbuf("z%d_%d" % (t, jh), [P, P], BF16)
            nc.vector.scalar_tensor_tensor(z[t, jh][:], ub[t][:, jh * P : (jh + 1) * P], gs_t[:, t : t + 1],
                                           sg[t][:, jh * P : (jh + 1) * P], ALU.mult, ALU.mult)

        def turn(t0, jh, copy):
            bank = ps.tile([P, 2, P], BF16, name="turn%d_%d" % (t0, jh), tag="bank_h", bufs=4)
            for i in range(2):
                nc.tensor.transpose(bank[:, i, :], z[t0 + i, jh][:], ident_b[:])
            copy(z_turned[:, jh, :, 32 * t0 : 32 * t0 + 64],
                 bank[:].rearrange("j i r -> j (i r)").bitcast(F32).rearrange("j (p u) -> j u p", u=2))

        pair_up(0, h_ps[0])
        dw1a = sbuf("dw1a", [P, HALF], U32, tag="pairs0")
        gather(dw1a[:], dw_tab, l_k1[:, hc : 2 * hc])
        pair_up(1, h_ps[1])
        dw1b = sbuf("dw1b", [P, 2 * HALF], U32, tag="h1")
        gather(dw1b[:, 0:HALF], dw_tab, l_k2[:, hc : 2 * hc])
        gather(dw1b[:, HALF : 2 * HALF], dw_tab, l_k3[:, hc : 2 * hc])
        dw1 = (dw1a[:], dw1b[:, 0:HALF], dw1b[:, HALF : 2 * HALF])
        h_ps2 = [ps.tile([P, S], F32, name="h_ps%d" % t, tag="bank_h", bufs=4) for t in (2, 3)]
        for a in range(3):
            for u in range(2):
                c = a * HALF + u * P
                mx(h_ps2[u][:], dw1[a][:, u * P : (u + 1) * P], plane2[:, c : c + P],
                   xw[:, a * S : (a + 1) * S], plane1[:, a * S : (a + 1) * S], a == 0, a == 2)

        put_back(0)
        picked3 = sbuf("picked3", [P, 2 * H + S], U8, tag="ranked0")
        gather(picked3[:, 0:H], ds_tab, l_k4[:])
        gather(picked3[:, H : 2 * H], ds_tab, l_k5[:])
        gather(picked3[:, 2 * H : 2 * H + S], xs_tab, l_two[:])
        place_scale_rows(nc.sync, plane3, picked3)
        l_n6 = load_list("l_n6", n6)
        l_n7 = load_list("l_n7", n7)
        put_back(1)
        xw_two = sbuf("xw_two", [P, S], U32, tag="ranked1")
        gather(xw_two[:], xw_tab, l_two[:])
        pair_up(2, h_ps2[0])
        pair_up(3, h_ps2[1])
        dw4 = sbuf("dw4", [P, H], U32, tag="pairs2")
        gather(dw4[:], dw_tab, l_k4[:])
        sg[0] = sbuf("sg0", [P, S], F32, tag="h2")
        sg[1] = sbuf("sg1", [P, S], F32, tag="h3")
        for jh in range(2):
            for t in (0, 1):
                gate(t, jh)
                weigh(t, jh)
        for jh in range(2):
            turn(0, jh, nc.vector.tensor_copy)
        dw5 = sbuf("dw5", [P, H], U32, tag="h3")
        gather(dw5[:], dw_tab, l_k5[:])
        put_back(2)
        put_back(3)
        sg[2] = sbuf("sg2", [P, S], F32)
        sg[3] = sbuf("sg3", [P, S], F32)
        for jh in range(2):
            for t in (2, 3):
                gate(t, jh)
                weigh(t, jh)
        turn(2, 0, nc.vector.tensor_copy)
        turn(2, 1, nc.scalar.copy)

        def deal_scales(half, tag):
            scales = sbuf("dealt_s%d" % half, [P, 2, 2, P], U8, tag=tag)
            nc.vector.tensor_copy(scales[:].rearrange("p a t m -> p a m t"),
                                  plane3[:, 0 : 2 * H].rearrange("p (a m t) -> p a m t", a=2, t=4)[:, :, :, 2 * half : 2 * half + 2])
            return scales

        def deal_words(half, tag):
            words = sbuf("dealt_w%d" % half, [P, 2, 2, P], U32, tag=tag)
            for a, picked in ((1, dw5), (0, dw4)):
                nc.vector.tensor_copy(words[:, a, :, :].rearrange("p t m -> p m t"),
                                      picked[:].rearrange("p (m t) -> p m t", t=4)[:, :, 2 * half : 2 * half + 2])
            return words

        z_in = [sbuf("z_in%d" % jh, [P, P, 4], BF16) for jh in range(2)]
        z_w = sbuf("z_w", [P, S], U32)
        z_s = sbuf("z_s", [P, S], U8)
        for jh in range(2):
            back = ps.tile([P, 2, P], F32, name="back%d" % jh, tag="bank_h", bufs=4)
            for u in range(2):
                nc.tensor.transpose(back[:, u, :], z_turned[:, jh, u, :], ident_f[:])
            nc.scalar.copy(z_in[jh][:].bitcast(F32), back[:].rearrange("p u j -> p j u"))
        scales0 = deal_scales(0, "sg3")
        words0 = deal_words(0, "ub3")
        for jh in range(2):
            cols = slice(jh * P, (jh + 1) * P)
            nc.vector.quantize_mx(out=z_w[:, cols].bitcast(FP8X4), scales=z_s[:, cols],
                                  in_=z_in[jh][:].rearrange("p j t -> p (j t)"))
        h2_ps = [ps.tile([P, S], F32, name="h2_ps%d" % t) for t in range(4)]

        def second_products(half, words, scales):
            for i in range(2):
                mx(h2_ps[2 * half + i][:], words[:, 1, i, :], scales[:, 1, i, :],
                   xw_two[:], plane3[:, 2 * H : 2 * H + S], True, False)
            for jh in range(2):
                cols = slice(jh * P, (jh + 1) * P)
                for i in range(2):
                    mx(h2_ps[2 * half + i][:, cols], words[:, 0, i, :], scales[:, 0, i, :], z_w[:, cols], z_s[:, cols], False, jh == 1)

        y_in = sbuf("y_in", [P, S, 4], BF16)
        out_rows = out_0.rearrange("(p t) j -> p t j", t=4)
        ys = []
        largest = []

        def pair_up_again(t):
            h2 = sbuf("h2_%d" % t, [P, S], F32)
            if t == 0:
                nc.scalar.activation(h2[:], h2_ps[t][:], ACT.Copy, scale=SIXTEENTH)
            else:
                nc.vector.tensor_scalar(h2[:], h2_ps[t][:], SIXTEENTH, None, ALU.mult)
            pairs2 = sbuf("pairs2_%d" % t, [P, 2 * W], F32)
            nc.scalar.activation(pairs2[:, 0:W], h2[:].indirect(l_n6[:]), ACT.Copy)
            nc.scalar.activation(pairs2[:, W : 2 * W], h2[:].indirect(l_n7[:]), ACT.Copy)
            y = sbuf("y%d" % t, [P, S], F32)
            nc.vector.tensor_copy(y[:], h2[:])
            big = sbuf("big%d" % t, [P, W], F32)
            nc.vector.tensor_tensor(big[:], pairs2[:, 0:W], pairs2[:, W : 2 * W], ALU.max)
            ys.append(y)
            largest.append(big)

        second_products(0, words0, scales0)
        words1 = deal_words(1, "z_in1")
        pair_up_again(0)
        pair_up_again(1)
        scales1 = deal_scales(1, "sg3")
        second_products(1, words1, scales1)
        pair_up_again(2)
        pair_up_again(3)
        for t in range(4):
            nc.scalar.activation(ys[t][:].indirect(l_n6[:]), largest[t][:], ACT.Copy)
            for cols in ([slice(0, S)] if t < 3 else [slice(0, P), slice(P, S)]):
                nc.vector.tensor_copy(y_in[:, cols, t], ys[t][:, cols])
            nc.sync.dma_start(out_rows[:, t, :], ys[t][:])
        y_w = sbuf("y_w", [P, S], U32)
        y_s = sbuf("y_s", [P, S], U8)
        for cols in (slice(0, P), slice(P, S)):
            nc.vector.quantize_mx(out=y_w[:, cols].bitcast(FP8X4), scales=y_s[:, cols], in_=y_in[:, cols, :].rearrange("p j t -> p (j t)"))
            nc.sync.dma_start(out_1[0].rearrange("p n t -> p (n t)").bitcast(I32)[:, cols], y_w[:, cols].bitcast(I32))
        for q in range(4):
            eng = nc.scalar if q % 2 == 0 else nc.sync
            eng.dma_start(out_2[0][4 * q : 4 * q + 4, :].bitcast(I32), y_s[32 * q : 32 * q + 4, :].bitcast(I32))
